import numpy as np
import ml_dtypes


def mxq(x, axis, fmt="e4m3"):
    dtype, down = {"e4m3": (ml_dtypes.float8_e4m3fn, 7), "e5m2": (ml_dtypes.float8_e5m2, 14)}[fmt]
    v = np.moveaxis(np.asarray(x, np.float32).astype(ml_dtypes.bfloat16).astype(np.float64), axis, -1)
    blocks = v.reshape(v.shape[:-1] + (-1, 32))
    amax = np.abs(blocks).max(-1, keepdims=True)
    byte = np.maximum(np.where(amax > 0, np.frexp(amax)[1] - 1 + 127, 0) - down, 1)
    scale = np.exp2(byte - 127.0)
    codes = (blocks / scale).astype(np.float32).astype(dtype).astype(np.float64)
    return np.moveaxis((codes * scale).reshape(v.shape), -1, axis)


WIDE = False


def mx_kscale(k):
    if not WIDE:
        return np.ones(k)
    levels = np.array([10, -10, 5, -5, 0])
    if k % 512:
        return np.exp2(np.random.permutation(np.resize(levels, k // 32))).repeat(32)
    a = np.empty((k // 512, 16))
    for p in range(k // 512):
        a[p, :8] = np.random.permutation(np.resize(levels, 8))
        for g in range(8):
            far = levels[np.abs(levels - a[p, g]) >= 10]
            a[p, g + 8] = far[np.random.randint(len(far))]
    return np.exp2(a.ravel()).repeat(32)


def f64(x):
    return np.asarray(x).astype(np.float64)


def striped(idx):
    return np.tile(idx.reshape(-1, 16).T, (8, 1)).astype(np.uint16)


def unstriped(offs):
    return offs[:16].T.reshape(-1).astype(np.int64)


def striped8(idx):
    return np.concatenate([x.reshape(-1, 16).T for x in idx]).astype(np.uint16)


def runs(offs, k):
    lists = np.stack([offs[16 * r : 16 * r + 16].T.reshape(-1) for r in range(8)]).astype(np.int64)
    return lists[np.arange(k) % 512 // 64]


def pack_weight(w):
    k, n = w.shape
    w = f64(np.asarray(w, np.float32).astype(ml_dtypes.bfloat16)).reshape(k // 32, 32, n)
    amax = np.abs(w).max(1)
    byte = np.clip(np.where(amax > 0, np.frexp(amax)[1] - 1 + 127 - 7, 1), 1, 254)
    scaled = (w * np.exp2(127.0 - byte)[:, None, :]).reshape(k, n).astype(np.float32)
    words = np.ascontiguousarray(scaled.reshape(k // 512, 128, 4, n).transpose(0, 1, 3, 2)).astype(ml_dtypes.float8_e4m3fn).view(np.uint8)
    return words, np.ascontiguousarray(byte.astype(np.uint8).reshape(k // 512, 16, n))


def unpack_weight(words, scales):
    g, p, n, _ = words.shape
    vals = np.ascontiguousarray(words).view(ml_dtypes.float8_e4m3fn).astype(np.float64) * np.repeat(np.exp2(scales.astype(np.float64) - 127.0), 8, axis=1)[..., None]
    return vals.transpose(0, 1, 3, 2).reshape(g * 512, n)


E2M1 = np.array([0.0, 0.5, 1.0, 1.5, 2.0, 3.0, 4.0, 6.0, -0.0, -0.5, -1.0, -1.5, -2.0, -3.0, -4.0, -6.0])


def pack_fp4(w):
    k, n = w.shape
    w = f64(np.asarray(w, np.float32).astype(ml_dtypes.bfloat16)).reshape(k // 32, 32, n)
    amax = np.abs(w).max(1)
    mant, ex = np.frexp(amax / 6.0)
    byte = np.clip(np.where(amax > 0, np.where(mant > 0.5, ex, ex - 1) + 127, 1), 1, 254)
    scaled = (w * np.exp2(127.0 - byte)[:, None, :]).reshape(k, n).astype(np.float32)
    c = np.ascontiguousarray(scaled.reshape(k // 512, 128, 4, n).transpose(0, 1, 3, 2)).astype(ml_dtypes.float4_e2m1fn).view(np.uint8) & 0xF
    words = (c[..., 0::2] | (c[..., 1::2] << 4)).reshape(k // 512, 128, 2 * n)
    return np.ascontiguousarray(words), np.ascontiguousarray(byte.astype(np.uint8).reshape(k // 512, 16, n))


def unpack_fp4(words, scales):
    g, _, n = scales.shape
    words = np.ascontiguousarray(words).reshape(g, 128, n, 2)
    nib = np.empty((g, 128, n, 4), np.uint8)
    nib[..., 0::2] = words & 0xF
    nib[..., 1::2] = words >> 4
    vals = E2M1[nib] * np.repeat(np.exp2(scales.astype(np.float64) - 127.0), 8, axis=1)[..., None]
    return vals.transpose(0, 1, 3, 2).reshape(g * 512, n)


def planes(y):
    n, m = y.shape
    v = y.astype(np.float32).astype(ml_dtypes.bfloat16).astype(np.float64).reshape(n // 32, 32, m)
    top = np.abs(v).max(1)
    byte = np.clip(np.where(top > 0, np.frexp(top)[1] - 1 + 127 - 7, 1), 1, 254)
    codes = (v * np.exp2(127.0 - byte)[:, None, :]).reshape(n, m).astype(np.float32).astype(ml_dtypes.float8_e4m3fn).view(np.uint8)
    words = codes.reshape(n // 512, 128, 4, m).transpose(0, 1, 3, 2)
    return np.ascontiguousarray(words), np.ascontiguousarray(byte.astype(np.uint8).reshape(n // 512, 16, m))


K, T, S, V, H, W = 512, 2048, 512, 512, 512, 256


def setup_inputs():
    n = np.random.standard_normal
    s = mx_kscale(K)[:, None]
    u = mx_kscale(S)
    packed_xT = pack_weight(n((K, T)) * s)
    packed_w1 = pack_fp4(n((K, H)) / np.sqrt(K) / s)
    packed_w2 = pack_fp4(n((K, H)) / np.sqrt(K) / s)
    packed_w3 = pack_fp4(n((K, H)) / np.sqrt(K) / s)
    perm = np.stack([np.random.permutation(V) for _ in range(8)])
    return {
        "x_words": packed_xT[0],
        "x_scales": packed_xT[1],
        "w1_words": packed_w1[0],
        "w1_scales": packed_w1[1],
        "w2_words": packed_w2[0],
        "w2_scales": packed_w2[1],
        "w3_words": packed_w3[0],
        "w3_scales": packed_w3[1],
        "ga": (np.random.uniform(0.5, 1.5, (H, 1)) * u[:, None]).astype(np.float32),
        "gb": (np.random.uniform(0.5, 1.5, (H, 1)) / u[:, None]).astype(np.float32),
        "offs": striped(np.random.permutation(T)[:S]),
        "two": striped(np.random.permutation(T)[:S]),
        "n1": striped8(np.stack([np.random.permutation(S) for _ in range(8)])),
        "n2": striped8(np.stack([np.random.permutation(S) for _ in range(8)])),
        "three": striped(np.random.permutation(T)[:V]),
        "n3": striped8(perm[:, :W]),
        "n4": striped8(perm[:, W:]),
        "n5": striped8(np.stack([np.random.permutation(V) for _ in range(8)])),
        "n6": striped8(np.stack([np.random.permutation(V) for _ in range(8)])),
    }


def reference(x_words, x_scales, w1_words, w1_scales, w2_words, w2_scales, w3_words, w3_scales, ga, gb, offs, two, n1, n2, three, n3, n4, n5, n6):
    xq = unpack_weight(x_words, x_scales)[:, unstriped(offs)]
    y = unpack_fp4(w1_words, w1_scales).T @ xq
    x_two = unpack_weight(x_words, x_scales)[:, unstriped(two)]
    d = unpack_fp4(w2_words, w2_scales).T @ x_two
    z = f64(ga) * ((y - (y[np.arange(H)[:, None], runs(n1, H)])) / (np.abs(d) + np.abs(d[np.arange(H)[:, None], runs(n2, H)]) + 0.5))
    x_three = unpack_weight(x_words, x_scales)[:, unstriped(three)]
    b = unpack_fp4(w3_words, w3_scales).T @ x_three
    pa = b[np.arange(H)[:, None], runs(n3, H)]
    pb = b[np.arange(H)[:, None], runs(n4, H)]
    rb = pa - pb
    ra = 0.75 * (pa + pb)
    ds = np.zeros((H, V))
    ds[np.arange(H)[:, None], runs(n3, H)] = ra
    dt = ds.copy()
    dt[np.arange(H)[:, None], runs(n4, H)] = rb
    z2 = f64(gb) * dt
    s = 0.0625 * ((mxq(z, 0, "e4m3").T @ mxq(z2, 0, "e4m3")))
    out_0 = (s[np.arange(S)[:, None], runs(n5, S)]) * (s[np.arange(S)[:, None], runs(n6, S)])
    return (out_0,) + planes(out_0)

@@ -1,0 +1,263 @@
+from contextlib import ExitStack
+
+import concourse.mybir as mybir
+from concourse.masks import make_identity
+
+K, T, S, V, H, W = 512, 2048, 512, 512, 512, 256
+FLOPS = 2 * K * H * (S + S + V) + 2 * H * S * V
+
+F32 = mybir.dt.float32
+BF16 = mybir.dt.bfloat16
+I32 = mybir.dt.int32
+U32 = mybir.dt.uint32
+U16 = mybir.dt.uint16
+U8 = mybir.dt.uint8
+FP8X4 = mybir.dt.float8_e4m3fn_x4
+FP4X4 = mybir.dt.float4_e2m1fn_x4
+ACT = mybir.ActivationFunctionType
+ALU = mybir.AluOpType
+
+P = 128
+PACK = 4
+QUADS = 4
+FIRST = 384
+
+
+def tile_picked_twknormbhaarprod_none_po_kernel(
+    tc, x_words, x_scales, w1_words, w1_scales, w2_words, w2_scales, w3_words, w3_scales,
+    ga, gb, offs, two, n1, n2, three, n3, n4, n5, n6, out_0, out_1, out_2,
+):
+    nc = tc.nc
+    with ExitStack() as ctx:
+        keep = ctx.enter_context(tc.tile_pool(name="keep", bufs=1))
+        psum = ctx.enter_context(tc.psum_pool(name="psum", bufs=8))
+
+        def sb(name, shape, dtype):
+            return keep.tile(shape, dtype, name=name, align_bytes=64)
+
+        def load_list(name, src):
+            tile = sb(name, list(src.shape), U16)
+            nc.sync.dma_start(tile[:], src)
+            return tile
+
+        def load_scale_rows(plane, src):
+            for q in range(QUADS):
+                nc.sync.dma_start(plane[32 * q : 32 * q + 4, :].bitcast(I32), src[0, 4 * q : 4 * q + 4, :].bitcast(I32))
+
+        xs = sb("xs", [P, T], U8)
+        nc.vector.memset(xs[:].bitcast(I32), 0)
+        ws_raw = {}
+        for name in ("w2", "w1", "w3"):
+            ws_raw[name] = sb(name + "_scales_raw", [P, H], U8)
+            nc.vector.memset(ws_raw[name][:].bitcast(I32), 0)
+        warm = sb("warm", [P, 2], F32)
+        nc.gpsimd.memset(warm[:, 0:1], 1.0)
+        nc.scalar.activation(warm[:, 1:2], warm[:, 0:1], ACT.Abs_reciprocal_sqrt)
+        g_rows = sb("g_rows", [P, P], F32)
+        nc.gpsimd.memset(g_rows[:], 0.0)
+        ident = sb("ident", [P, P], F32)
+        make_identity(nc, ident[:])
+
+        d_win = [sb("d_win%d" % t, [P, 2 * S], F32) for t in range(PACK)]
+        y_win = [sb("y_win%d" % t, [P, 2 * S], F32) for t in range(PACK)]
+        d_last = sb("d_last", [P, S], F32)
+        y_last = sb("y_last", [P, S], F32)
+        nc.vector.memset(d_win[0][:, S:], 0.0)
+        nc.vector.memset(y_win[0][:, S:], 0.0)
+        d_plain = [d_win[t + 1][:, S:] for t in range(PACK - 1)] + [d_last[:]]
+        y_plain = [y_win[t + 1][:, S:] for t in range(PACK - 1)] + [y_last[:]]
+
+        load_scale_rows(xs, x_scales)
+        two_t = load_list("two_t", two)
+        xw = sb("xw", [P, T], U32)
+        nc.sync.dma_start(xw[:].bitcast(I32), x_words[0].rearrange("p n r -> p (n r)").bitcast(I32))
+        offs_t = load_list("offs_t", offs)
+        three_t = load_list("three_t", three)
+        ww_raw = {}
+
+        def load_weight(name, words, scales):
+            ww_raw[name] = sb(name + "_words_raw", [P, 2 * H], U8)
+            nc.sync.dma_start(ww_raw[name][:].bitcast(I32), words[0].bitcast(I32))
+            load_scale_rows(ws_raw[name], scales)
+
+        load_weight("w2", w2_words, w2_scales)
+        for first, g in ((0, ga), (PACK, gb)):
+            nc.sync.dma_start(
+                g_rows[first : first + PACK, :].rearrange("t (b q) -> t b q", q=8),
+                g.rearrange("(b t q) o -> t b (q o)", t=PACK, q=8),
+            )
+        n2_t = load_list("n2_t", n2)
+        load_weight("w1", w1_words, w1_scales)
+        load_weight("w3", w3_words, w3_scales)
+        n1_t = load_list("n1_t", n1)
+        n3_t = load_list("n3_t", n3)
+        n4_t = load_list("n4_t", n4)
+        n5_t = load_list("n5_t", n5)
+        n6_t = load_list("n6_t", n6)
+
+        g_ps = psum.tile([P, 512], F32, name="bank")
+        nc.tensor.transpose(g_ps[:, 0:P], g_rows[:], ident[:])
+        g_cols = sb("g_cols", [P, 2 * PACK], F32)
+        nc.scalar.mul(g_cols[:, 0:PACK], g_ps[:, 0:PACK], -1.0)
+        nc.scalar.copy(g_cols[:, PACK:], g_ps[:, PACK : 2 * PACK])
+
+        streams = (("w2", two_t), ("w1", offs_t), ("w3", three_t))
+        picked_s, picked_w, wd, sd = {}, {}, {}, {}
+        for name, lst in streams:
+            picked_s[name] = sb(name + "_xs", [P, S], U8)
+            nc.vector.tensor_copy(picked_s[name][:], xs[:].indirect(lst[:]))
+        for name, lst in streams:
+            picked_w[name] = sb(name + "_xw", [P, S], U32)
+            nc.vector.tensor_copy(picked_w[name][:], xw[:].indirect(lst[:]))
+            wd[name] = sb(name + "_words", [P, 2 * H], U8)
+            nc.vector.tensor_copy(
+                wd[name][:].bitcast(I32).rearrange("p (t b e) -> p t b e", t=PACK, e=4),
+                ww_raw[name][:].bitcast(I32).rearrange("p (b t e) -> p t b e", t=PACK, e=4),
+            )
+            sd[name] = sb(name + "_scales", [P, H], U8)
+            nc.vector.tensor_copy(
+                sd[name][:].bitcast(I32).rearrange("p (t b e) -> p t b e", t=PACK, e=2),
+                ws_raw[name][:].bitcast(I32).rearrange("p (b t e) -> p t b e", t=PACK, e=2),
+            )
+
+        def project(name, t):
+            bank = psum.tile([P, 512], F32, name="bank")
+            nc.tensor.matmul_mx(
+                out=bank[:],
+                lhsT=wd[name][:, 2 * P * t : 2 * P * (t + 1)].bitcast(FP4X4),
+                lhsT_scale=sd[name][:, P * t : P * (t + 1)],
+                rhs=picked_w[name][:].bitcast(FP8X4),
+                rhs_scale=picked_s[name][:],
+                start=True,
+                stop=True,
+            )
+            return bank
+
+        for t in range(PACK):
+            bank = project("w2", t)
+            nc.scalar.activation(d_win[t][:, :S], bank[:], ACT.Abs)
+            nc.scalar.activation(d_plain[t], bank[:], ACT.Abs)
+        for t in range(PACK):
+            bank = project("w1", t)
+            nc.scalar.activation(y_win[t][:, :S], bank[:], ACT.Copy, scale=g_cols[:, t : t + 1])
+            nc.scalar.activation(y_plain[t], bank[:], ACT.Copy, scale=g_cols[:, t : t + 1])
+        b_win = [sb("b_win%d" % t, [P, V], F32) for t in range(PACK)]
+        for t in range(PACK):
+            bank = project("w3", t)
+            nc.scalar.activation(b_win[t][:], bank[:], ACT.Copy, scale=g_cols[:, PACK + t : PACK + t + 1])
+
+        den = sb("den", [P, PACK, S], F32)
+        num = sb("num", [P, PACK, S], F32)
+        for t in range(PACK):
+            nc.vector.tensor_tensor(den[:, t, :], d_win[t][:].indirect(n2_t[:]), d_plain[t], ALU.add)
+        for t in range(PACK):
+            nc.vector.tensor_tensor(num[:, t, :], y_win[t][:].indirect(n1_t[:]), y_plain[t], ALU.subtract)
+
+        pa = sb("pa", [P, PACK, W], F32)
+        pb_neg = sb("pb_neg", [P, PACK, W], F32)
+        pa_part = sb("pa_part", [P, PACK, W], F32)
+        pb_part = sb("pb_part", [P, PACK, W], F32)
+        for t in range(PACK):
+            nc.vector.tensor_copy(pa[:, t, :], b_win[t][:].indirect(n3_t[:]))
+            nc.vector.tensor_scalar(pb_neg[:, t, :], b_win[t][:].indirect(n4_t[:]), -1.0, 0.0, ALU.mult, ALU.add)
+
+        root = sb("root", [P, PACK, S], F32)
+        nc.scalar.activation(root[:], den[:], ACT.Abs_reciprocal_sqrt, bias=0.5)
+        for t in range(PACK):
+            nc.scalar.mul(pa_part[:, t, :], pa[:, t, :], 0.75)
+            nc.scalar.mul(pb_part[:, t, :], pb_neg[:, t, :], -0.75)
+        inv = sb("inv", [P, PACK, P, PACK], F32)
+        num_d = sb("num_d", [P, PACK, P, PACK], F32)
+        nc.scalar.activation(
+            inv[:].rearrange("p u m t -> p m t u"), root[:].rearrange("p t (m u) -> p m t u", u=PACK), ACT.Square
+        )
+        nc.scalar.copy(num_d[:].rearrange("p u m t -> p m t u"), num[:].rearrange("p t (m u) -> p m t u", u=PACK))
+
+        dt = [sb("dt%d" % t, [P, V], F32) for t in range(PACK)]
+        z2_b = sb("z2_b", [P, V, PACK], BF16)
+        for t0 in range(0, PACK, 2):
+            for t in (t0, t0 + 1):
+                nc.vector.tensor_tensor(dt[t][:].indirect(n4_t[:]), pa[:, t, :], pb_neg[:, t, :], ALU.add)
+            for t in (t0, t0 + 1):
+                nc.vector.tensor_tensor(dt[t][:].indirect(n3_t[:]), pa_part[:, t, :], pb_part[:, t, :], ALU.add)
+                nc.scalar.copy(z2_b[:, :, t], dt[t][:])
+
+        z_b = sb("z_b", [P, PACK, P * PACK], BF16)
+        z_w = sb("z_w", [P, S], U32)
+        z_s = sb("z_s", [P, S], U8)
+        z2_w = sb("z2_w", [P, V], U32)
+        z2_s = sb("z2_s", [P, V], U8)
+
+        def z_product(u):
+            nc.vector.tensor_tensor(
+                z_b[:, u, :], num_d[:, u].rearrange("p m t -> p (m t)"), inv[:, u].rearrange("p m t -> p (m t)"), ALU.mult
+            )
+
+        def z_quantize(u):
+            nc.vector.quantize_mx(z_w[:, P * u : P * (u + 1)].bitcast(FP8X4), z_s[:, P * u : P * (u + 1)], z_b[:, u, :])
+
+        z_product(0)
+        z_product(1)
+        z_quantize(0)
+        z_quantize(1)
+        nc.vector.quantize_mx(z2_w[:].bitcast(FP8X4), z2_s[:], z2_b[:].rearrange("p v t -> p (v t)"))
+        z_product(2)
+        z_product(3)
+        z_quantize(2)
+        z_quantize(3)
+
+        s_win = [sb("s_win%d" % u, [P, V], F32) for u in range(PACK)]
+        for u in range(PACK):
+            bank = psum.tile([P, 512], F32, name="bank")
+            nc.tensor.matmul_mx(
+                out=bank[:],
+                lhsT=z_w[:, P * u : P * (u + 1)].bitcast(FP8X4),
+                lhsT_scale=z_s[:, P * u : P * (u + 1)],
+                rhs=z2_w[:].bitcast(FP8X4),
+                rhs_scale=z2_s[:],
+                start=True,
+                stop=True,
+            )
+            nc.scalar.mul(s_win[u][:], bank[:], 0.0625)
+
+        s5 = sb("s5", [P, PACK, V], F32)
+        res = sb("res", [P, PACK, V], F32)
+        res_b = sb("res_b", [P, V, PACK], BF16)
+        res_w = sb("res_w", [P, V], U32)
+        res_s = sb("res_s", [P, V], U8)
+        out_rows = out_0.rearrange("(p u) v -> p u v", u=PACK)
+        out_words = out_1[0].rearrange("p v r -> p (v r)").bitcast(I32)
+
+        def products(c0, c1):
+            for u0 in range(0, PACK, 2):
+                for u in (u0, u0 + 1):
+                    nc.vector.tensor_copy(s5[:, u, c0:c1], s_win[u][:].indirect(n5_t[:, c0 // 16 : c1 // 16]))
+                for u in (u0, u0 + 1):
+                    nc.vector.tensor_tensor(
+                        res[:, u, c0:c1], s_win[u][:].indirect(n6_t[:, c0 // 16 : c1 // 16]), s5[:, u, c0:c1], ALU.mult
+                    )
+            nc.sync.dma_start(out_rows[:, :, c0:c1], res[:, :, c0:c1])
+
+        def weave_views(c0, c1):
+            return (
+                res_b[:, c0:c1, :].rearrange("p (c i) u -> p c u i", i=4),
+                res[:, :, c0:c1].rearrange("p u (c i) -> p c u i", i=4),
+            )
+
+        def res_quantize(c0, c1):
+            nc.vector.quantize_mx(
+                res_w[:, c0:c1].bitcast(FP8X4), res_s[:, c0:c1], res_b[:, c0:c1, :].rearrange("p v u -> p (v u)")
+            )
+
+        products(0, FIRST)
+        nc.scalar.copy(*weave_views(0, FIRST))
+        products(FIRST, V)
+        res_quantize(0, 256)
+        res_quantize(256, FIRST)
+        nc.vector.tensor_copy(*weave_views(FIRST, V))
+        nc.sync.dma_start(out_words[:, 0:FIRST], res_w[:, 0:FIRST].bitcast(I32))
+        res_quantize(FIRST, V)
+        nc.sync.dma_start(out_words[:, FIRST:], res_w[:, FIRST:].bitcast(I32))
+        for q in range(QUADS):
+            queue = nc.scalar if q % 2 else nc.sync
+            queue.dma_start(out_2[0, 4 * q : 4 * q + 4, :].bitcast(I32), res_s[32 * q : 32 * q + 4, :].bitcast(I32))

@@ -32,8 +32,8 @@ def tile_picked_twknormbhaarprod_none_po_kernel(
         keep = ctx.enter_context(tc.tile_pool(name="keep", bufs=1))
         psum = ctx.enter_context(tc.psum_pool(name="psum", bufs=8))
 
-        def sb(name, shape, dtype):
-            return keep.tile(shape, dtype, name=name, align_bytes=64)
+        def sb(name, shape, dtype, tag=None):
+            return keep.tile(shape, dtype, name=name, tag=tag or name, align_bytes=64)
 
         def load_list(name, src):
             tile = sb(name, list(src.shape), U16)
@@ -45,6 +45,7 @@ def tile_picked_twknormbhaarprod_none_po_kernel(
                 nc.sync.dma_start(plane[32 * q : 32 * q + 4, :].bitcast(I32), src[0, 4 * q : 4 * q + 4, :].bitcast(I32))
 
         xs = sb("xs", [P, T], U8)
+        xs_rows = sb("xs_rows", [P, T], U8)
         nc.vector.memset(xs[:].bitcast(I32), 0)
         ws_raw = {}
         for name in ("w2", "w1", "w3"):
@@ -67,12 +68,14 @@ def tile_picked_twknormbhaarprod_none_po_kernel(
         d_plain = [d_win[t + 1][:, S:] for t in range(PACK - 1)] + [d_last[:]]
         y_plain = [y_win[t + 1][:, S:] for t in range(PACK - 1)] + [y_last[:]]
 
-        load_scale_rows(xs, x_scales)
+        load_scale_rows(xs_rows, x_scales)
         two_t = load_list("two_t", two)
-        xw = sb("xw", [P, T], U32)
-        nc.sync.dma_start(xw[:].bitcast(I32), x_words[0].rearrange("p n r -> p (n r)").bitcast(I32))
         offs_t = load_list("offs_t", offs)
         three_t = load_list("three_t", three)
+        xw = sb("xw", [P, T], U32)
+        nc.sync.dma_start(xw[:].bitcast(I32), x_words[0].rearrange("p n r -> p (n r)").bitcast(I32))
+        for q in range(QUADS):
+            nc.vector.tensor_copy(xs[32 * q : 32 * q + 4, :].bitcast(I32), xs_rows[32 * q : 32 * q + 4, :].bitcast(I32))
         ww_raw = {}
 
         def load_weight(name, words, scales):
@@ -106,9 +109,13 @@ def tile_picked_twknormbhaarprod_none_po_kernel(
         for name, lst in streams:
             picked_s[name] = sb(name + "_xs", [P, S], U8)
             nc.vector.tensor_copy(picked_s[name][:], xs[:].indirect(lst[:]))
+        first_w = sb("first_xw", [P, S], U32)
+        picked_w["w2"] = first_w[:]
         for name, lst in streams:
-            picked_w[name] = sb(name + "_xw", [P, S], U32)
-            nc.vector.tensor_copy(picked_w[name][:], xw[:].indirect(lst[:]))
+            if name == "w1":
+                later_w = sb("later_xw", [P, S + V], U32, tag="w2_scales_raw")
+                picked_w["w1"], picked_w["w3"] = later_w[:, :S], later_w[:, S:]
+            nc.vector.tensor_copy(picked_w[name], xw[:].indirect(lst[:]))
             wd[name] = sb(name + "_words", [P, 2 * H], U8)
             nc.vector.tensor_copy(
                 wd[name][:].bitcast(I32).rearrange("p (t b e) -> p t b e", t=PACK, e=4),
@@ -126,7 +133,7 @@ def tile_picked_twknormbhaarprod_none_po_kernel(
                 out=bank[:],
                 lhsT=wd[name][:, 2 * P * t : 2 * P * (t + 1)].bitcast(FP4X4),
                 lhsT_scale=sd[name][:, P * t : P * (t + 1)],
-                rhs=picked_w[name][:].bitcast(FP8X4),
+                rhs=picked_w[name].bitcast(FP8X4),
                 rhs_scale=picked_s[name][:],
                 start=True,
                 stop=True,
@@ -155,17 +162,14 @@ def tile_picked_twknormbhaarprod_none_po_kernel(
 
         pa = sb("pa", [P, PACK, W], F32)
         pb_neg = sb("pb_neg", [P, PACK, W], F32)
-        pa_part = sb("pa_part", [P, PACK, W], F32)
-        pb_part = sb("pb_part", [P, PACK, W], F32)
+        pa_part = [sb("pa_part%d" % t, [P, W], F32) for t in range(PACK)]
+        pb_part = [sb("pb_part%d" % t, [P, W], F32) for t in range(PACK)]
         for t in range(PACK):
             nc.vector.tensor_copy(pa[:, t, :], b_win[t][:].indirect(n3_t[:]))
             nc.vector.tensor_scalar(pb_neg[:, t, :], b_win[t][:].indirect(n4_t[:]), -1.0, 0.0, ALU.mult, ALU.add)
 
         root = sb("root", [P, PACK, S], F32)
         nc.scalar.activation(root[:], den[:], ACT.Abs_reciprocal_sqrt, bias=0.5)
-        for t in range(PACK):
-            nc.scalar.mul(pa_part[:, t, :], pa[:, t, :], 0.75)
-            nc.scalar.mul(pb_part[:, t, :], pb_neg[:, t, :], -0.75)
         inv = sb("inv", [P, PACK, P, PACK], F32)
         num_d = sb("num_d", [P, PACK, P, PACK], F32)
         nc.scalar.activation(
@@ -173,16 +177,20 @@ def tile_picked_twknormbhaarprod_none_po_kernel(
         )
         nc.scalar.copy(num_d[:].rearrange("p u m t -> p m t u"), num[:].rearrange("p t (m u) -> p m t u", u=PACK))
 
+        for t in range(PACK):
+            nc.scalar.mul(pa_part[t][:], pa[:, t, :], 0.75)
+            nc.scalar.mul(pb_part[t][:], pb_neg[:, t, :], -0.75)
+
         dt = [sb("dt%d" % t, [P, V], F32) for t in range(PACK)]
         z2_b = sb("z2_b", [P, V, PACK], BF16)
-        for t0 in range(0, PACK, 2):
-            for t in (t0, t0 + 1):
-                nc.vector.tensor_tensor(dt[t][:].indirect(n4_t[:]), pa[:, t, :], pb_neg[:, t, :], ALU.add)
-            for t in (t0, t0 + 1):
-                nc.vector.tensor_tensor(dt[t][:].indirect(n3_t[:]), pa_part[:, t, :], pb_part[:, t, :], ALU.add)
-                nc.scalar.copy(z2_b[:, :, t], dt[t][:])
+        for t in range(PACK):
+            nc.vector.tensor_tensor(dt[t][:].indirect(n4_t[:]), pa[:, t, :], pb_neg[:, t, :], ALU.add)
+        for t in range(PACK):
+            nc.vector.tensor_tensor(dt[t][:].indirect(n3_t[:]), pa_part[t][:], pb_part[t][:], ALU.add)
+            nc.scalar.copy(z2_b[:, :, t], dt[t][:])
 
-        z_b = sb("z_b", [P, PACK, P * PACK], BF16)
+        z2_flat = z2_b[:].rearrange("p v t -> p (v t)")
+        z_b = [pa_part[PACK - 1][:].bitcast(BF16), pb_part[PACK - 1][:].bitcast(BF16), z2_flat[:, 0:S], z2_flat[:, S : 2 * S]]
         z_w = sb("z_w", [P, S], U32)
         z_s = sb("z_s", [P, S], U8)
         z2_w = sb("z2_w", [P, V], U32)
@@ -190,17 +198,17 @@ def tile_picked_twknormbhaarprod_none_po_kernel(
 
         def z_product(u):
             nc.vector.tensor_tensor(
-                z_b[:, u, :], num_d[:, u].rearrange("p m t -> p (m t)"), inv[:, u].rearrange("p m t -> p (m t)"), ALU.mult
+                z_b[u], num_d[:, u].rearrange("p m t -> p (m t)"), inv[:, u].rearrange("p m t -> p (m t)"), ALU.mult
             )
 
         def z_quantize(u):
-            nc.vector.quantize_mx(z_w[:, P * u : P * (u + 1)].bitcast(FP8X4), z_s[:, P * u : P * (u + 1)], z_b[:, u, :])
+            nc.vector.quantize_mx(z_w[:, P * u : P * (u + 1)].bitcast(FP8X4), z_s[:, P * u : P * (u + 1)], z_b[u])
 
         z_product(0)
         z_product(1)
         z_quantize(0)
         z_quantize(1)
-        nc.vector.quantize_mx(z2_w[:].bitcast(FP8X4), z2_s[:], z2_b[:].rearrange("p v t -> p (v t)"))
+        nc.vector.quantize_mx(z2_w[:].bitcast(FP8X4), z2_s[:], z2_flat)
         z_product(2)
         z_product(3)
         z_quantize(2)

@@ -65,6 +65,9 @@ def tile_picked_twknormbhaarprod_none_po_kernel(
         y_last = sb("y_last", [P, S], F32)
         nc.vector.memset(d_win[0][:, S:], 0.0)
         nc.vector.memset(y_win[0][:, S:], 0.0)
+        s_win = [sb("s_win%d" % u, [P, 2 * V if u < 2 else V], F32) for u in range(PACK)]
+        for u in range(2):
+            nc.gpsimd.memset(s_win[u][:, V:], 0.0)
         d_plain = [d_win[t + 1][:, S:] for t in range(PACK - 1)] + [d_last[:]]
         y_plain = [y_win[t + 1][:, S:] for t in range(PACK - 1)] + [y_last[:]]
 
@@ -113,16 +116,16 @@ def tile_picked_twknormbhaarprod_none_po_kernel(
         picked_w["w2"] = first_w[:]
         for name, lst in streams:
             if name == "w1":
-                later_w = sb("later_xw", [P, S + V], U32, tag="w2_scales_raw")
+                later_w = sb("later_xw", [P, S + V], U32)
                 picked_w["w1"], picked_w["w3"] = later_w[:, :S], later_w[:, S:]
             nc.vector.tensor_copy(picked_w[name], xw[:].indirect(lst[:]))
             wd[name] = sb(name + "_words", [P, 2 * H], U8)
-            nc.vector.tensor_copy(
+            nc.gpsimd.tensor_copy(
                 wd[name][:].bitcast(I32).rearrange("p (t b e) -> p t b e", t=PACK, e=4),
                 ww_raw[name][:].bitcast(I32).rearrange("p (b t e) -> p t b e", t=PACK, e=4),
             )
             sd[name] = sb(name + "_scales", [P, H], U8)
-            nc.vector.tensor_copy(
+            nc.gpsimd.tensor_copy(
                 sd[name][:].bitcast(I32).rearrange("p (t b e) -> p t b e", t=PACK, e=2),
                 ws_raw[name][:].bitcast(I32).rearrange("p (b t e) -> p t b e", t=PACK, e=2),
             )
@@ -190,7 +193,7 @@ def tile_picked_twknormbhaarprod_none_po_kernel(
             nc.scalar.copy(z2_b[:, :, t], dt[t][:])
 
         z2_flat = z2_b[:].rearrange("p v t -> p (v t)")
-        z_b = [pa_part[PACK - 1][:].bitcast(BF16), pb_part[PACK - 1][:].bitcast(BF16), z2_flat[:, 0:S], z2_flat[:, S : 2 * S]]
+        z_b = [pa_part[PACK - 1][:].bitcast(BF16), pb_part[PACK - 1][:].bitcast(BF16), z2_flat[:, 2 * S : 3 * S], z2_flat[:, 3 * S :]]
         z_w = sb("z_w", [P, S], U32)
         z_s = sb("z_s", [P, S], U8)
         z2_w = sb("z2_w", [P, V], U32)
@@ -208,63 +211,66 @@ def tile_picked_twknormbhaarprod_none_po_kernel(
         z_product(1)
         z_quantize(0)
         z_quantize(1)
-        nc.vector.quantize_mx(z2_w[:].bitcast(FP8X4), z2_s[:], z2_flat)
+        for c0 in (0, V // 2):
+            cols = slice(c0, c0 + V // 2)
+            nc.vector.quantize_mx(z2_w[:, cols].bitcast(FP8X4), z2_s[:, cols], z2_flat[:, PACK * c0 : PACK * (c0 + V // 2)])
         z_product(2)
         z_product(3)
         z_quantize(2)
         z_quantize(3)
 
-        s_win = [sb("s_win%d" % u, [P, V], F32) for u in range(PACK)]
-        for u in range(PACK):
+        for u, c0, c1 in [(0, 0, V // 2), (0, V // 2, V)] + [(u, 0, V) for u in range(1, PACK)]:
             bank = psum.tile([P, 512], F32, name="bank")
             nc.tensor.matmul_mx(
-                out=bank[:],
+                out=bank[:, : c1 - c0],
                 lhsT=z_w[:, P * u : P * (u + 1)].bitcast(FP8X4),
                 lhsT_scale=z_s[:, P * u : P * (u + 1)],
-                rhs=z2_w[:].bitcast(FP8X4),
-                rhs_scale=z2_s[:],
+                rhs=z2_w[:, c0:c1].bitcast(FP8X4),
+                rhs_scale=z2_s[:, c0:c1],
                 start=True,
                 stop=True,
             )
-            nc.scalar.mul(s_win[u][:], bank[:], 0.0625)
+            nc.scalar.mul(s_win[u][:, c0:c1], bank[:, : c1 - c0], 0.0625)
 
         s5 = sb("s5", [P, PACK, V], F32)
         res = sb("res", [P, PACK, V], F32)
-        res_b = sb("res_b", [P, V, PACK], BF16)
+        res_b = sb("res_b", [P, FIRST, PACK], BF16)
         res_w = sb("res_w", [P, V], U32)
         res_s = sb("res_s", [P, V], U8)
         out_rows = out_0.rearrange("(p u) v -> p u v", u=PACK)
         out_words = out_1[0].rearrange("p v r -> p (v r)").bitcast(I32)
 
-        def products(c0, c1):
-            for u0 in range(0, PACK, 2):
-                for u in (u0, u0 + 1):
-                    nc.vector.tensor_copy(s5[:, u, c0:c1], s_win[u][:].indirect(n5_t[:, c0 // 16 : c1 // 16]))
-                for u in (u0, u0 + 1):
-                    nc.vector.tensor_tensor(
-                        res[:, u, c0:c1], s_win[u][:].indirect(n6_t[:, c0 // 16 : c1 // 16]), s5[:, u, c0:c1], ALU.mult
-                    )
-            nc.sync.dma_start(out_rows[:, :, c0:c1], res[:, :, c0:c1])
+        def products(u0, c0, c1):
+            for u in (u0, u0 + 1):
+                nc.vector.tensor_copy(s5[:, u, c0:c1], s_win[u][:].indirect(n5_t[:, c0 // 16 : c1 // 16]))
+            for u in (u0, u0 + 1):
+                nc.vector.tensor_tensor(
+                    res[:, u, c0:c1], s_win[u][:].indirect(n6_t[:, c0 // 16 : c1 // 16]), s5[:, u, c0:c1], ALU.mult
+                )
+            nc.sync.dma_start(out_rows[:, u0 : u0 + 2, c0:c1], res[:, u0 : u0 + 2, c0:c1])
 
-        def weave_views(c0, c1):
-            return (
-                res_b[:, c0:c1, :].rearrange("p (c i) u -> p c u i", i=4),
-                res[:, :, c0:c1].rearrange("p u (c i) -> p c u i", i=4),
+        def weave_first(u0):
+            nc.scalar.copy(
+                res_b[:, :, u0 : u0 + 2].rearrange("p (c i) u -> p c u i", i=4),
+                res[:, u0 : u0 + 2, 0:FIRST].rearrange("p u (c i) -> p c u i", i=4),
             )
 
-        def res_quantize(c0, c1):
-            nc.vector.quantize_mx(
-                res_w[:, c0:c1].bitcast(FP8X4), res_s[:, c0:c1], res_b[:, c0:c1, :].rearrange("p v u -> p (v u)")
-            )
+        def res_quantize(c0, c1, woven):
+            nc.vector.quantize_mx(res_w[:, c0:c1].bitcast(FP8X4), res_s[:, c0:c1], woven.rearrange("p v u -> p (v u)"))
 
-        products(0, FIRST)
-        nc.scalar.copy(*weave_views(0, FIRST))
-        products(FIRST, V)
-        res_quantize(0, 256)
-        res_quantize(256, FIRST)
-        nc.vector.tensor_copy(*weave_views(FIRST, V))
+        products(0, 0, V)
+        weave_first(0)
+        products(2, 0, FIRST)
+        weave_first(2)
+        products(2, FIRST, V)
+        res_quantize(256, FIRST, res_b[:, 256:FIRST, :])
+        res_quantize(0, 256, res_b[:, 0:256, :])
         nc.sync.dma_start(out_words[:, 0:FIRST], res_w[:, 0:FIRST].bitcast(I32))
-        res_quantize(FIRST, V)
+        last_b = res_b[:, 0 : V - FIRST, :]
+        nc.vector.tensor_copy(
+            last_b.rearrange("p (c i) u -> p c u i", i=4), res[:, :, FIRST:].rearrange("p u (c i) -> p c u i", i=4)
+        )
+        res_quantize(FIRST, V, last_b)
         nc.sync.dma_start(out_words[:, FIRST:], res_w[:, FIRST:].bitcast(I32))
         for q in range(QUADS):
             queue = nc.scalar if q % 2 else nc.sync

@@ -110,8 +110,9 @@ def tile_picked_twknormbhaarprod_none_po_kernel(
         streams = (("w2", two_t), ("w1", offs_t), ("w3", three_t))
         picked_s, picked_w, wd, sd = {}, {}, {}, {}
         for name, lst in streams:
-            picked_s[name] = sb(name + "_xs", [P, S], U8)
-            nc.vector.tensor_copy(picked_s[name][:], xs[:].indirect(lst[:]))
+            if name != "w3":
+                picked_s[name] = sb(name + "_xs", [P, S], U8)
+                nc.vector.tensor_copy(picked_s[name][:], xs[:].indirect(lst[:]))
         first_w = sb("first_xw", [P, S], U32)
         picked_w["w2"] = first_w[:]
         for name, lst in streams:
@@ -129,6 +130,9 @@ def tile_picked_twknormbhaarprod_none_po_kernel(
                 sd[name][:].bitcast(I32).rearrange("p (t b e) -> p t b e", t=PACK, e=2),
                 ws_raw[name][:].bitcast(I32).rearrange("p (b t e) -> p t b e", t=PACK, e=2),
             )
+
+        picked_s["w3"] = sb("w3_xs", [P, S], U8, tag="w2_scales_raw")
+        nc.vector.tensor_copy(picked_s["w3"][:], xs[:].indirect(three_t[:]))
 
         def project(name, t):
             bank = psum.tile([P, 512], F32, name="bank")
@@ -190,7 +194,8 @@ def tile_picked_twknormbhaarprod_none_po_kernel(
             nc.vector.tensor_tensor(dt[t][:].indirect(n4_t[:]), pa[:, t, :], pb_neg[:, t, :], ALU.add)
         for t in range(PACK):
             nc.vector.tensor_tensor(dt[t][:].indirect(n3_t[:]), pa_part[t][:], pb_part[t][:], ALU.add)
-            nc.scalar.copy(z2_b[:, :, t], dt[t][:])
+            for c0, c1 in ((0, V // 2), (V // 2, V)) if t == PACK - 1 else ((0, V),):
+                nc.scalar.copy(z2_b[:, c0:c1, t], dt[t][:, c0:c1])
 
         z2_flat = z2_b[:].rearrange("p v t -> p (v t)")
         z_b = [pa_part[PACK - 1][:].bitcast(BF16), pb_part[PACK - 1][:].bitcast(BF16), z2_flat[:, 2 * S : 3 * S], z2_flat[:, 3 * S :]]
@@ -234,7 +239,7 @@ def tile_picked_twknormbhaarprod_none_po_kernel(
 
         s5 = sb("s5", [P, PACK, V], F32)
         res = sb("res", [P, PACK, V], F32)
-        res_b = sb("res_b", [P, FIRST, PACK], BF16)
+        res_b = sb("res_b", [P, V, PACK], BF16)
         res_w = sb("res_w", [P, V], U32)
         res_s = sb("res_s", [P, V], U8)
         out_rows = out_0.rearrange("(p u) v -> p u v", u=PACK)
@@ -249,28 +254,24 @@ def tile_picked_twknormbhaarprod_none_po_kernel(
                 )
             nc.sync.dma_start(out_rows[:, u0 : u0 + 2, c0:c1], res[:, u0 : u0 + 2, c0:c1])
 
-        def weave_first(u0):
+        def weave(u0, c0, c1):
             nc.scalar.copy(
-                res_b[:, :, u0 : u0 + 2].rearrange("p (c i) u -> p c u i", i=4),
-                res[:, u0 : u0 + 2, 0:FIRST].rearrange("p u (c i) -> p c u i", i=4),
+                res_b[:, c0:c1, u0 : u0 + 2].rearrange("p (c i) u -> p c u i", i=4),
+                res[:, u0 : u0 + 2, c0:c1].rearrange("p u (c i) -> p c u i", i=4),
             )
 
-        def res_quantize(c0, c1, woven):
-            nc.vector.quantize_mx(res_w[:, c0:c1].bitcast(FP8X4), res_s[:, c0:c1], woven.rearrange("p v u -> p (v u)"))
+        def res_quantize(c0, c1):
+            nc.vector.quantize_mx(
+                res_w[:, c0:c1].bitcast(FP8X4), res_s[:, c0:c1], res_b[:, c0:c1, :].rearrange("p v u -> p (v u)")
+            )
 
-        products(0, 0, V)
-        weave_first(0)
-        products(2, 0, FIRST)
-        weave_first(2)
-        products(2, FIRST, V)
-        res_quantize(256, FIRST, res_b[:, 256:FIRST, :])
-        res_quantize(0, 256, res_b[:, 0:256, :])
+        for u0, c0, c1 in ((0, 0, V), (2, 0, FIRST), (2, FIRST, V)):
+            products(u0, c0, c1)
+            weave(u0, c0, c1)
+        res_quantize(0, 256)
+        res_quantize(256, FIRST)
         nc.sync.dma_start(out_words[:, 0:FIRST], res_w[:, 0:FIRST].bitcast(I32))
-        last_b = res_b[:, 0 : V - FIRST, :]
-        nc.vector.tensor_copy(
-            last_b.rearrange("p (c i) u -> p c u i", i=4), res[:, :, FIRST:].rearrange("p u (c i) -> p c u i", i=4)
-        )
-        res_quantize(FIRST, V, last_b)
+        res_quantize(FIRST, V)
         nc.sync.dma_start(out_words[:, FIRST:], res_w[:, FIRST:].bitcast(I32))
         for q in range(QUADS):
             queue = nc.scalar if q % 2 else nc.sync

@@ -18,8 +18,12 @@ ACT = mybir.ActivationFunctionType
 ALU = mybir.AluOpType
 
 P = 128
-PACK = 4
+TILES = 4
 QUADS = 4
+RUN = 8
+BANK = 512
+BANKS = 8
+LIST = 16
 FIRST = 384
 
 
@@ -30,7 +34,7 @@ def tile_picked_twknormbhaarprod_none_po_kernel(
     nc = tc.nc
     with ExitStack() as ctx:
         keep = ctx.enter_context(tc.tile_pool(name="keep", bufs=1))
-        psum = ctx.enter_context(tc.psum_pool(name="psum", bufs=8))
+        psum = ctx.enter_context(tc.psum_pool(name="psum", bufs=BANKS))
 
         def sb(name, shape, dtype, tag=None):
             return keep.tile(shape, dtype, name=name, tag=tag or name, align_bytes=64)
@@ -45,32 +49,29 @@ def tile_picked_twknormbhaarprod_none_po_kernel(
                 nc.sync.dma_start(plane[32 * q : 32 * q + 4, :].bitcast(I32), src[0, 4 * q : 4 * q + 4, :].bitcast(I32))
 
         xs = sb("xs", [P, T], U8)
-        xs_rows = sb("xs_rows", [P, T], U8)
         nc.vector.memset(xs[:].bitcast(I32), 0)
-        ws_raw = {}
+        w_scales_raw = {}
         for name in ("w2", "w1", "w3"):
-            ws_raw[name] = sb(name + "_scales_raw", [P, H], U8)
-            nc.vector.memset(ws_raw[name][:].bitcast(I32), 0)
-        warm = sb("warm", [P, 2], F32)
-        nc.gpsimd.memset(warm[:, 0:1], 1.0)
-        nc.scalar.activation(warm[:, 1:2], warm[:, 0:1], ACT.Abs_reciprocal_sqrt)
-        g_rows = sb("g_rows", [P, P], F32)
-        nc.gpsimd.memset(g_rows[:], 0.0)
+            w_scales_raw[name] = sb(name + "_scales_raw", [P, H], U8)
+            nc.vector.memset(w_scales_raw[name][:].bitcast(I32), 0)
+        gain_rows = sb("gain_rows", [P, P], F32)
+        nc.gpsimd.memset(gain_rows[:], 0.0)
         ident = sb("ident", [P, P], F32)
         make_identity(nc, ident[:])
 
-        d_win = [sb("d_win%d" % t, [P, 2 * S], F32) for t in range(PACK)]
-        y_win = [sb("y_win%d" % t, [P, 2 * S], F32) for t in range(PACK)]
+        d_win = [sb("d_win%d" % t, [P, 2 * S], F32) for t in range(TILES)]
+        y_win = [sb("y_win%d" % t, [P, 2 * S], F32) for t in range(TILES)]
         d_last = sb("d_last", [P, S], F32)
         y_last = sb("y_last", [P, S], F32)
         nc.vector.memset(d_win[0][:, S:], 0.0)
         nc.vector.memset(y_win[0][:, S:], 0.0)
-        s_win = [sb("s_win%d" % u, [P, 2 * V if u < 2 else V], F32) for u in range(PACK)]
+        s_win = [sb("s_win%d" % u, [P, 2 * V if u < 2 else V], F32) for u in range(TILES)]
         for u in range(2):
             nc.gpsimd.memset(s_win[u][:, V:], 0.0)
-        d_plain = [d_win[t + 1][:, S:] for t in range(PACK - 1)] + [d_last[:]]
-        y_plain = [y_win[t + 1][:, S:] for t in range(PACK - 1)] + [y_last[:]]
+        d_plain = [d_win[t + 1][:, S:] for t in range(TILES - 1)] + [d_last[:]]
+        y_plain = [y_win[t + 1][:, S:] for t in range(TILES - 1)] + [y_last[:]]
 
+        xs_rows = sb("xs_rows", [P, T], U8)
         load_scale_rows(xs_rows, x_scales)
         two_t = load_list("two_t", two)
         offs_t = load_list("offs_t", offs)
@@ -79,18 +80,18 @@ def tile_picked_twknormbhaarprod_none_po_kernel(
         nc.sync.dma_start(xw[:].bitcast(I32), x_words[0].rearrange("p n r -> p (n r)").bitcast(I32))
         for q in range(QUADS):
             nc.vector.tensor_copy(xs[32 * q : 32 * q + 4, :].bitcast(I32), xs_rows[32 * q : 32 * q + 4, :].bitcast(I32))
-        ww_raw = {}
+        w_words_raw = {}
 
         def load_weight(name, words, scales):
-            ww_raw[name] = sb(name + "_words_raw", [P, 2 * H], U8)
-            nc.sync.dma_start(ww_raw[name][:].bitcast(I32), words[0].bitcast(I32))
-            load_scale_rows(ws_raw[name], scales)
+            w_words_raw[name] = sb(name + "_words_raw", [P, 2 * H], U8)
+            nc.sync.dma_start(w_words_raw[name][:].bitcast(I32), words[0].bitcast(I32))
+            load_scale_rows(w_scales_raw[name], scales)
 
         load_weight("w2", w2_words, w2_scales)
-        for first, g in ((0, ga), (PACK, gb)):
+        for first_row, gain in ((0, ga), (TILES, gb)):
             nc.sync.dma_start(
-                g_rows[first : first + PACK, :].rearrange("t (b q) -> t b q", q=8),
-                g.rearrange("(b t q) o -> t b (q o)", t=PACK, q=8),
+                gain_rows[first_row : first_row + TILES, :].rearrange("t (g e) -> t g e", e=RUN),
+                gain.rearrange("(g t e) o -> t g (e o)", t=TILES, e=RUN),
             )
         n2_t = load_list("n2_t", n2)
         load_weight("w1", w1_words, w1_scales)
@@ -101,45 +102,42 @@ def tile_picked_twknormbhaarprod_none_po_kernel(
         n5_t = load_list("n5_t", n5)
         n6_t = load_list("n6_t", n6)
 
-        g_ps = psum.tile([P, 512], F32, name="bank")
-        nc.tensor.transpose(g_ps[:, 0:P], g_rows[:], ident[:])
-        g_cols = sb("g_cols", [P, 2 * PACK], F32)
-        nc.scalar.mul(g_cols[:, 0:PACK], g_ps[:, 0:PACK], -1.0)
-        nc.scalar.copy(g_cols[:, PACK:], g_ps[:, PACK : 2 * PACK])
+        gain_bank = psum.tile([P, BANK], F32, name="bank")
+        nc.tensor.transpose(gain_bank[:, 0:P], gain_rows[:], ident[:])
+        gains = sb("gains", [P, 2 * TILES], F32)
+        nc.scalar.copy(gains[:], gain_bank[:, 0 : 2 * TILES])
 
-        streams = (("w2", two_t), ("w1", offs_t), ("w3", three_t))
-        picked_s, picked_w, wd, sd = {}, {}, {}, {}
-        for name, lst in streams:
-            if name != "w3":
-                picked_s[name] = sb(name + "_xs", [P, S], U8)
-                nc.vector.tensor_copy(picked_s[name][:], xs[:].indirect(lst[:]))
-        first_w = sb("first_xw", [P, S], U32)
-        picked_w["w2"] = first_w[:]
-        for name, lst in streams:
-            if name == "w1":
-                later_w = sb("later_xw", [P, S + V], U32)
-                picked_w["w1"], picked_w["w3"] = later_w[:, :S], later_w[:, S:]
-            nc.vector.tensor_copy(picked_w[name], xw[:].indirect(lst[:]))
-            wd[name] = sb(name + "_words", [P, 2 * H], U8)
-            nc.gpsimd.tensor_copy(
-                wd[name][:].bitcast(I32).rearrange("p (t b e) -> p t b e", t=PACK, e=4),
-                ww_raw[name][:].bitcast(I32).rearrange("p (b t e) -> p t b e", t=PACK, e=4),
-            )
-            sd[name] = sb(name + "_scales", [P, H], U8)
-            nc.gpsimd.tensor_copy(
-                sd[name][:].bitcast(I32).rearrange("p (t b e) -> p t b e", t=PACK, e=2),
-                ws_raw[name][:].bitcast(I32).rearrange("p (b t e) -> p t b e", t=PACK, e=2),
-            )
+        picked_s, picked_w, w_words, w_scales = {}, {}, {}, {}
 
-        picked_s["w3"] = sb("w3_xs", [P, S], U8, tag="w2_scales_raw")
-        nc.vector.tensor_copy(picked_s["w3"][:], xs[:].indirect(three_t[:]))
+        def pick_scales(name, lst, tag=None):
+            picked_s[name] = sb(name + "_xs", [P, S], U8, tag=tag)
+            nc.vector.tensor_copy(picked_s[name][:], xs[:].indirect(lst[:]))
+
+        pick_scales("w2", two_t)
+        pick_scales("w1", offs_t)
+        first_xw = sb("first_xw", [P, S], U32)
+        later_xw = sb("later_xw", [P, S + V], U32)
+        for name, lst, picked in (("w2", two_t, first_xw[:]), ("w1", offs_t, later_xw[:, :S]), ("w3", three_t, later_xw[:, S:])):
+            picked_w[name] = picked
+            nc.vector.tensor_copy(picked, xw[:].indirect(lst[:]))
+            w_words[name] = sb(name + "_words", [P, 2 * H], U8)
+            nc.gpsimd.tensor_copy(
+                w_words[name][:].bitcast(I32).rearrange("p (t g c) -> p t g c", t=TILES, c=RUN // 2),
+                w_words_raw[name][:].bitcast(I32).rearrange("p (g t c) -> p t g c", t=TILES, c=RUN // 2),
+            )
+            w_scales[name] = sb(name + "_scales", [P, H], U8)
+            nc.gpsimd.tensor_copy(
+                w_scales[name][:].bitcast(I32).rearrange("p (t g c) -> p t g c", t=TILES, c=RUN // 4),
+                w_scales_raw[name][:].bitcast(I32).rearrange("p (g t c) -> p t g c", t=TILES, c=RUN // 4),
+            )
+        pick_scales("w3", three_t, tag="w2_scales_raw")
 
         def project(name, t):
-            bank = psum.tile([P, 512], F32, name="bank")
+            bank = psum.tile([P, BANK], F32, name="bank")
             nc.tensor.matmul_mx(
                 out=bank[:],
-                lhsT=wd[name][:, 2 * P * t : 2 * P * (t + 1)].bitcast(FP4X4),
-                lhsT_scale=sd[name][:, P * t : P * (t + 1)],
+                lhsT=w_words[name][:, 2 * P * t : 2 * P * (t + 1)].bitcast(FP4X4),
+                lhsT_scale=w_scales[name][:, P * t : P * (t + 1)],
                 rhs=picked_w[name].bitcast(FP8X4),
                 rhs_scale=picked_s[name][:],
                 start=True,
@@ -147,85 +145,79 @@ def tile_picked_twknormbhaarprod_none_po_kernel(
             )
             return bank
 
-        for t in range(PACK):
+        for t in range(TILES):
             bank = project("w2", t)
             nc.scalar.activation(d_win[t][:, :S], bank[:], ACT.Abs)
             nc.scalar.activation(d_plain[t], bank[:], ACT.Abs)
-        for t in range(PACK):
+        for t in range(TILES):
             bank = project("w1", t)
-            nc.scalar.activation(y_win[t][:, :S], bank[:], ACT.Copy, scale=g_cols[:, t : t + 1])
-            nc.scalar.activation(y_plain[t], bank[:], ACT.Copy, scale=g_cols[:, t : t + 1])
-        b_win = [sb("b_win%d" % t, [P, V], F32) for t in range(PACK)]
-        for t in range(PACK):
+            nc.scalar.activation(y_win[t][:, :S], bank[:], ACT.Copy, scale=gains[:, t : t + 1])
+            nc.scalar.activation(y_plain[t], bank[:], ACT.Copy, scale=gains[:, t : t + 1])
+        b_win = [sb("b_win%d" % t, [P, V], F32) for t in range(TILES)]
+        for t in range(TILES):
             bank = project("w3", t)
-            nc.scalar.activation(b_win[t][:], bank[:], ACT.Copy, scale=g_cols[:, PACK + t : PACK + t + 1])
+            nc.scalar.activation(b_win[t][:], bank[:], ACT.Copy, scale=gains[:, TILES + t : TILES + t + 1])
 
-        den = sb("den", [P, PACK, S], F32)
-        num = sb("num", [P, PACK, S], F32)
-        for t in range(PACK):
-            nc.vector.tensor_tensor(den[:, t, :], d_win[t][:].indirect(n2_t[:]), d_plain[t], ALU.add)
-        for t in range(PACK):
-            nc.vector.tensor_tensor(num[:, t, :], y_win[t][:].indirect(n1_t[:]), y_plain[t], ALU.subtract)
+        sizes = sb("sizes", [P, TILES, S], F32)
+        diff = sb("diff", [P, TILES, S], F32)
+        for t in range(TILES):
+            nc.vector.tensor_tensor(sizes[:, t, :], d_win[t][:].indirect(n2_t[:]), d_plain[t], ALU.add)
+        for t in range(TILES):
+            nc.vector.tensor_tensor(diff[:, t, :], y_win[t][:].indirect(n1_t[:]), y_plain[t], ALU.subtract)
 
-        pa = sb("pa", [P, PACK, W], F32)
-        pb_neg = sb("pb_neg", [P, PACK, W], F32)
-        pa_part = [sb("pa_part%d" % t, [P, W], F32) for t in range(PACK)]
-        pb_part = [sb("pb_part%d" % t, [P, W], F32) for t in range(PACK)]
-        for t in range(PACK):
+        pa = sb("pa", [P, TILES, W], F32, tag="gains")
+        pb_neg = sb("pb_neg", [P, TILES, W], F32)
+        pa_part = [sb("pa_part%d" % t, [P, W], F32) for t in range(TILES)]
+        pb_part = [sb("pb_part%d" % t, [P, W], F32) for t in range(TILES)]
+        for t in range(TILES):
             nc.vector.tensor_copy(pa[:, t, :], b_win[t][:].indirect(n3_t[:]))
             nc.vector.tensor_scalar(pb_neg[:, t, :], b_win[t][:].indirect(n4_t[:]), -1.0, 0.0, ALU.mult, ALU.add)
 
-        root = sb("root", [P, PACK, S], F32)
-        nc.scalar.activation(root[:], den[:], ACT.Abs_reciprocal_sqrt, bias=0.5)
-        inv = sb("inv", [P, PACK, P, PACK], F32)
-        num_d = sb("num_d", [P, PACK, P, PACK], F32)
+        root = sb("root", [P, TILES, S], F32)
+        nc.scalar.activation(root[:], sizes[:], ACT.Abs_reciprocal_sqrt, bias=0.5)
+        inv = sb("inv", [P, TILES, P, TILES], F32)
+        numer = sb("numer", [P, TILES, P, TILES], F32)
         nc.scalar.activation(
-            inv[:].rearrange("p u m t -> p m t u"), root[:].rearrange("p t (m u) -> p m t u", u=PACK), ACT.Square
+            inv[:].rearrange("p u m t -> p m t u"), root[:].rearrange("p t (m u) -> p m t u", u=TILES), ACT.Square
         )
-        nc.scalar.copy(num_d[:].rearrange("p u m t -> p m t u"), num[:].rearrange("p t (m u) -> p m t u", u=PACK))
+        nc.scalar.mul(numer[:].rearrange("p u m t -> p m t u"), diff[:].rearrange("p t (m u) -> p m t u", u=TILES), -1.0)
 
-        for t in range(PACK):
+        for t in range(TILES):
             nc.scalar.mul(pa_part[t][:], pa[:, t, :], 0.75)
             nc.scalar.mul(pb_part[t][:], pb_neg[:, t, :], -0.75)
 
-        dt = [sb("dt%d" % t, [P, V], F32) for t in range(PACK)]
-        z2_b = sb("z2_b", [P, V, PACK], BF16)
-        for t in range(PACK):
+        halves = ((0, V // 2), (V // 2, V))
+        dt = [sb("dt%d" % t, [P, V], F32) for t in range(TILES)]
+        z2_b = sb("z2_b", [P, V, TILES], BF16)
+        for t in range(TILES):
             nc.vector.tensor_tensor(dt[t][:].indirect(n4_t[:]), pa[:, t, :], pb_neg[:, t, :], ALU.add)
-        for t in range(PACK):
+        for t in range(TILES):
             nc.vector.tensor_tensor(dt[t][:].indirect(n3_t[:]), pa_part[t][:], pb_part[t][:], ALU.add)
-            for c0, c1 in ((0, V // 2), (V // 2, V)) if t == PACK - 1 else ((0, V),):
+            for c0, c1 in halves if t == TILES - 1 else ((0, V),):
                 nc.scalar.copy(z2_b[:, c0:c1, t], dt[t][:, c0:c1])
 
         z2_flat = z2_b[:].rearrange("p v t -> p (v t)")
-        z_b = [pa_part[PACK - 1][:].bitcast(BF16), pb_part[PACK - 1][:].bitcast(BF16), z2_flat[:, 2 * S : 3 * S], z2_flat[:, 3 * S :]]
+        z_b = [pa_part[TILES - 1][:].bitcast(BF16), pb_part[TILES - 1][:].bitcast(BF16), z2_flat[:, 2 * S : 3 * S], z2_flat[:, 3 * S :]]
         z_w = sb("z_w", [P, S], U32)
         z_s = sb("z_s", [P, S], U8)
         z2_w = sb("z2_w", [P, V], U32)
         z2_s = sb("z2_s", [P, V], U8)
 
-        def z_product(u):
-            nc.vector.tensor_tensor(
-                z_b[u], num_d[:, u].rearrange("p m t -> p (m t)"), inv[:, u].rearrange("p m t -> p (m t)"), ALU.mult
-            )
+        def make_z(u0):
+            for u in (u0, u0 + 1):
+                nc.vector.tensor_tensor(
+                    z_b[u], numer[:, u].rearrange("p m t -> p (m t)"), inv[:, u].rearrange("p m t -> p (m t)"), ALU.mult
+                )
+            for u in (u0, u0 + 1):
+                nc.vector.quantize_mx(z_w[:, P * u : P * (u + 1)].bitcast(FP8X4), z_s[:, P * u : P * (u + 1)], z_b[u])
 
-        def z_quantize(u):
-            nc.vector.quantize_mx(z_w[:, P * u : P * (u + 1)].bitcast(FP8X4), z_s[:, P * u : P * (u + 1)], z_b[u])
+        make_z(0)
+        for c0, c1 in halves:
+            nc.vector.quantize_mx(z2_w[:, c0:c1].bitcast(FP8X4), z2_s[:, c0:c1], z2_flat[:, TILES * c0 : TILES * c1])
+        make_z(2)
 
-        z_product(0)
-        z_product(1)
-        z_quantize(0)
-        z_quantize(1)
-        for c0 in (0, V // 2):
-            cols = slice(c0, c0 + V // 2)
-            nc.vector.quantize_mx(z2_w[:, cols].bitcast(FP8X4), z2_s[:, cols], z2_flat[:, PACK * c0 : PACK * (c0 + V // 2)])
-        z_product(2)
-        z_product(3)
-        z_quantize(2)
-        z_quantize(3)
-
-        for u, c0, c1 in [(0, 0, V // 2), (0, V // 2, V)] + [(u, 0, V) for u in range(1, PACK)]:
-            bank = psum.tile([P, 512], F32, name="bank")
+        for u, c0, c1 in [(0, c0, c1) for c0, c1 in halves] + [(u, 0, V) for u in range(1, TILES)]:
+            bank = psum.tile([P, BANK], F32, name="bank")
             nc.tensor.matmul_mx(
                 out=bank[:, : c1 - c0],
                 lhsT=z_w[:, P * u : P * (u + 1)].bitcast(FP8X4),
@@ -237,41 +229,35 @@ def tile_picked_twknormbhaarprod_none_po_kernel(
             )
             nc.scalar.mul(s_win[u][:, c0:c1], bank[:, : c1 - c0], 0.0625)
 
-        s5 = sb("s5", [P, PACK, V], F32)
-        res = sb("res", [P, PACK, V], F32)
-        res_b = sb("res_b", [P, V, PACK], BF16)
+        s5 = sb("s5", [P, TILES, V], F32)
+        res = sb("res", [P, TILES, V], F32)
+        res_b = sb("res_b", [P, V, TILES], BF16)
         res_w = sb("res_w", [P, V], U32)
         res_s = sb("res_s", [P, V], U8)
-        out_rows = out_0.rearrange("(p u) v -> p u v", u=PACK)
+        out_rows = out_0.rearrange("(p u) v -> p u v", u=TILES)
         out_words = out_1[0].rearrange("p v r -> p (v r)").bitcast(I32)
 
-        def products(u0, c0, c1):
+        for u0, c0, c1 in ((0, 0, V), (2, 0, FIRST), (2, FIRST, V)):
+            entries = slice(c0 // LIST, c1 // LIST)
             for u in (u0, u0 + 1):
-                nc.vector.tensor_copy(s5[:, u, c0:c1], s_win[u][:].indirect(n5_t[:, c0 // 16 : c1 // 16]))
+                nc.vector.tensor_copy(s5[:, u, c0:c1], s_win[u][:].indirect(n5_t[:, entries]))
             for u in (u0, u0 + 1):
-                nc.vector.tensor_tensor(
-                    res[:, u, c0:c1], s_win[u][:].indirect(n6_t[:, c0 // 16 : c1 // 16]), s5[:, u, c0:c1], ALU.mult
-                )
+                nc.vector.tensor_tensor(res[:, u, c0:c1], s_win[u][:].indirect(n6_t[:, entries]), s5[:, u, c0:c1], ALU.mult)
             nc.sync.dma_start(out_rows[:, u0 : u0 + 2, c0:c1], res[:, u0 : u0 + 2, c0:c1])
-
-        def weave(u0, c0, c1):
             nc.scalar.copy(
                 res_b[:, c0:c1, u0 : u0 + 2].rearrange("p (c i) u -> p c u i", i=4),
                 res[:, u0 : u0 + 2, c0:c1].rearrange("p u (c i) -> p c u i", i=4),
             )
 
-        def res_quantize(c0, c1):
+        def quantize_res(c0, c1):
             nc.vector.quantize_mx(
                 res_w[:, c0:c1].bitcast(FP8X4), res_s[:, c0:c1], res_b[:, c0:c1, :].rearrange("p v u -> p (v u)")
             )
 
-        for u0, c0, c1 in ((0, 0, V), (2, 0, FIRST), (2, FIRST, V)):
-            products(u0, c0, c1)
-            weave(u0, c0, c1)
-        res_quantize(0, 256)
-        res_quantize(256, FIRST)
+        quantize_res(0, V // 2)
+        quantize_res(V // 2, FIRST)
         nc.sync.dma_start(out_words[:, 0:FIRST], res_w[:, 0:FIRST].bitcast(I32))
-        res_quantize(FIRST, V)
+        quantize_res(FIRST, V)
         nc.sync.dma_start(out_words[:, FIRST:], res_w[:, FIRST:].bitcast(I32))
         for q in range(QUADS):
             queue = nc.scalar if q % 2 else nc.sync

from contextlib import ExitStack

import concourse.mybir as mybir
from concourse.masks import make_identity

K, T, S, V, H, W = 512, 2048, 512, 512, 512, 256
FLOPS = 2 * K * H * (S + S + V) + 2 * H * S * V

F32 = mybir.dt.float32
BF16 = mybir.dt.bfloat16
I32 = mybir.dt.int32
U32 = mybir.dt.uint32
U16 = mybir.dt.uint16
U8 = mybir.dt.uint8
FP8X4 = mybir.dt.float8_e4m3fn_x4
FP4X4 = mybir.dt.float4_e2m1fn_x4
ACT = mybir.ActivationFunctionType
ALU = mybir.AluOpType

P = 128
TILES = 4
QUADS = 4
RUN = 8
BANK = 512
BANKS = 8
LIST = 16
FIRST = 384


def tile_picked_twknormbhaarprod_none_po_kernel(
    tc, x_words, x_scales, w1_words, w1_scales, w2_words, w2_scales, w3_words, w3_scales,
    ga, gb, offs, two, n1, n2, three, n3, n4, n5, n6, out_0, out_1, out_2,
):
    nc = tc.nc
    with ExitStack() as ctx:
        keep = ctx.enter_context(tc.tile_pool(name="keep", bufs=1))
        psum = ctx.enter_context(tc.psum_pool(name="psum", bufs=BANKS))

        def sb(name, shape, dtype, tag=None):
            return keep.tile(shape, dtype, name=name, tag=tag or name, align_bytes=64)

        def load_list(name, src):
            tile = sb(name, list(src.shape), U16)
            nc.sync.dma_start(tile[:], src)
            return tile

        def load_scale_rows(plane, src):
            for q in range(QUADS):
                nc.sync.dma_start(plane[32 * q : 32 * q + 4, :].bitcast(I32), src[0, 4 * q : 4 * q + 4, :].bitcast(I32))

        xs = sb("xs", [P, T], U8)
        nc.vector.memset(xs[:].bitcast(I32), 0)
        w_scales_raw = {}
        for name in ("w2", "w1", "w3"):
            w_scales_raw[name] = sb(name + "_scales_raw", [P, H], U8)
            nc.vector.memset(w_scales_raw[name][:].bitcast(I32), 0)
        gain_rows = sb("gain_rows", [P, P], F32)
        nc.gpsimd.memset(gain_rows[:], 0.0)
        ident = sb("ident", [P, P], F32)
        make_identity(nc, ident[:])

        d_win = [sb("d_win%d" % t, [P, 2 * S], F32) for t in range(TILES)]
        y_win = [sb("y_win%d" % t, [P, 2 * S], F32) for t in range(TILES)]
        d_last = sb("d_last", [P, S], F32)
        y_last = sb("y_last", [P, S], F32)
        nc.vector.memset(d_win[0][:, S:], 0.0)
        nc.vector.memset(y_win[0][:, S:], 0.0)
        s_win = [sb("s_win%d" % u, [P, 2 * V if u < 2 else V], F32) for u in range(TILES)]
        for u in range(2):
            nc.gpsimd.memset(s_win[u][:, V:], 0.0)
        d_plain = [d_win[t + 1][:, S:] for t in range(TILES - 1)] + [d_last[:]]
        y_plain = [y_win[t + 1][:, S:] for t in range(TILES - 1)] + [y_last[:]]

        xs_rows = sb("xs_rows", [P, T], U8)
        load_scale_rows(xs_rows, x_scales)
        two_t = load_list("two_t", two)
        offs_t = load_list("offs_t", offs)
        three_t = load_list("three_t", three)
        xw = sb("xw", [P, T], U32)
        nc.sync.dma_start(xw[:].bitcast(I32), x_words[0].rearrange("p n r -> p (n r)").bitcast(I32))
        for q in range(QUADS):
            nc.vector.tensor_copy(xs[32 * q : 32 * q + 4, :].bitcast(I32), xs_rows[32 * q : 32 * q + 4, :].bitcast(I32))
        w_words_raw = {}

        def load_weight(name, words, scales):
            w_words_raw[name] = sb(name + "_words_raw", [P, 2 * H], U8)
            nc.sync.dma_start(w_words_raw[name][:].bitcast(I32), words[0].bitcast(I32))
            load_scale_rows(w_scales_raw[name], scales)

        load_weight("w2", w2_words, w2_scales)
        for first_row, gain in ((0, ga), (TILES, gb)):
            nc.sync.dma_start(
                gain_rows[first_row : first_row + TILES, :].rearrange("t (g e) -> t g e", e=RUN),
                gain.rearrange("(g t e) o -> t g (e o)", t=TILES, e=RUN),
            )
        n2_t = load_list("n2_t", n2)
        load_weight("w1", w1_words, w1_scales)
        load_weight("w3", w3_words, w3_scales)
        n1_t = load_list("n1_t", n1)
        n3_t = load_list("n3_t", n3)
        n4_t = load_list("n4_t", n4)
        n5_t = load_list("n5_t", n5)
        n6_t = load_list("n6_t", n6)

        gain_bank = psum.tile([P, BANK], F32, name="bank")
        nc.tensor.transpose(gain_bank[:, 0:P], gain_rows[:], ident[:])
        gains = sb("gains", [P, 2 * TILES], F32)
        nc.scalar.copy(gains[:], gain_bank[:, 0 : 2 * TILES])

        picked_s, picked_w, w_words, w_scales = {}, {}, {}, {}

        def pick_scales(name, lst, tag=None):
            picked_s[name] = sb(name + "_xs", [P, S], U8, tag=tag)
            nc.vector.tensor_copy(picked_s[name][:], xs[:].indirect(lst[:]))

        pick_scales("w2", two_t)
        pick_scales("w1", offs_t)
        first_xw = sb("first_xw", [P, S], U32)
        later_xw = sb("later_xw", [P, S + V], U32)
        for name, lst, picked in (("w2", two_t, first_xw[:]), ("w1", offs_t, later_xw[:, :S]), ("w3", three_t, later_xw[:, S:])):
            picked_w[name] = picked
            nc.vector.tensor_copy(picked, xw[:].indirect(lst[:]))
            w_words[name] = sb(name + "_words", [P, 2 * H], U8)
            nc.gpsimd.tensor_copy(
                w_words[name][:].bitcast(I32).rearrange("p (t g c) -> p t g c", t=TILES, c=RUN // 2),
                w_words_raw[name][:].bitcast(I32).rearrange("p (g t c) -> p t g c", t=TILES, c=RUN // 2),
            )
            w_scales[name] = sb(name + "_scales", [P, H], U8)
            nc.gpsimd.tensor_copy(
                w_scales[name][:].bitcast(I32).rearrange("p (t g c) -> p t g c", t=TILES, c=RUN // 4),
                w_scales_raw[name][:].bitcast(I32).rearrange("p (g t c) -> p t g c", t=TILES, c=RUN // 4),
            )
        pick_scales("w3", three_t, tag="w2_scales_raw")

        def project(name, t):
            bank = psum.tile([P, BANK], F32, name="bank")
            nc.tensor.matmul_mx(
                out=bank[:],
                lhsT=w_words[name][:, 2 * P * t : 2 * P * (t + 1)].bitcast(FP4X4),
                lhsT_scale=w_scales[name][:, P * t : P * (t + 1)],
                rhs=picked_w[name].bitcast(FP8X4),
                rhs_scale=picked_s[name][:],
                start=True,
                stop=True,
            )
            return bank

        for t in range(TILES):
            bank = project("w2", t)
            nc.scalar.activation(d_win[t][:, :S], bank[:], ACT.Abs)
            nc.scalar.activation(d_plain[t], bank[:], ACT.Abs)
        for t in range(TILES):
            bank = project("w1", t)
            nc.scalar.activation(y_win[t][:, :S], bank[:], ACT.Copy, scale=gains[:, t : t + 1])
            nc.scalar.activation(y_plain[t], bank[:], ACT.Copy, scale=gains[:, t : t + 1])
        b_win = [sb("b_win%d" % t, [P, V], F32) for t in range(TILES)]
        for t in range(TILES):
            bank = project("w3", t)
            nc.scalar.activation(b_win[t][:], bank[:], ACT.Copy, scale=gains[:, TILES + t : TILES + t + 1])

        sizes = sb("sizes", [P, TILES, S], F32)
        diff = sb("diff", [P, TILES, S], F32)
        for t in range(TILES):
            nc.vector.tensor_tensor(sizes[:, t, :], d_win[t][:].indirect(n2_t[:]), d_plain[t], ALU.add)
        for t in range(TILES):
            nc.vector.tensor_tensor(diff[:, t, :], y_win[t][:].indirect(n1_t[:]), y_plain[t], ALU.subtract)

        pa = sb("pa", [P, TILES, W], F32, tag="gains")
        pb_neg = sb("pb_neg", [P, TILES, W], F32)
        pa_part = [sb("pa_part%d" % t, [P, W], F32) for t in range(TILES)]
        pb_part = [sb("pb_part%d" % t, [P, W], F32) for t in range(TILES)]
        for t in range(TILES):
            nc.vector.tensor_copy(pa[:, t, :], b_win[t][:].indirect(n3_t[:]))
            nc.vector.tensor_scalar(pb_neg[:, t, :], b_win[t][:].indirect(n4_t[:]), -1.0, 0.0, ALU.mult, ALU.add)

        root = sb("root", [P, TILES, S], F32)
        nc.scalar.activation(root[:], sizes[:], ACT.Abs_reciprocal_sqrt, bias=0.5)
        inv = sb("inv", [P, TILES, P, TILES], F32)
        numer = sb("numer", [P, TILES, P, TILES], F32)
        nc.scalar.activation(
            inv[:].rearrange("p u m t -> p m t u"), root[:].rearrange("p t (m u) -> p m t u", u=TILES), ACT.Square
        )
        nc.scalar.mul(numer[:].rearrange("p u m t -> p m t u"), diff[:].rearrange("p t (m u) -> p m t u", u=TILES), -1.0)

        for t in range(TILES):
            nc.scalar.mul(pa_part[t][:], pa[:, t, :], 0.75)
            nc.scalar.mul(pb_part[t][:], pb_neg[:, t, :], -0.75)

        halves = ((0, V // 2), (V // 2, V))
        dt = [sb("dt%d" % t, [P, V], F32) for t in range(TILES)]
        z2_b = sb("z2_b", [P, V, TILES], BF16)
        for t in range(TILES):
            nc.vector.tensor_tensor(dt[t][:].indirect(n4_t[:]), pa[:, t, :], pb_neg[:, t, :], ALU.add)
        for t in range(TILES):
            nc.vector.tensor_tensor(dt[t][:].indirect(n3_t[:]), pa_part[t][:], pb_part[t][:], ALU.add)
            for c0, c1 in halves if t == TILES - 1 else ((0, V),):
                nc.scalar.copy(z2_b[:, c0:c1, t], dt[t][:, c0:c1])

        z2_flat = z2_b[:].rearrange("p v t -> p (v t)")
        z_b = [pa_part[TILES - 1][:].bitcast(BF16), pb_part[TILES - 1][:].bitcast(BF16), z2_flat[:, 2 * S : 3 * S], z2_flat[:, 3 * S :]]
        z_w = sb("z_w", [P, S], U32)
        z_s = sb("z_s", [P, S], U8)
        z2_w = sb("z2_w", [P, V], U32)
        z2_s = sb("z2_s", [P, V], U8)

        def make_z(u0):
            for u in (u0, u0 + 1):
                nc.vector.tensor_tensor(
                    z_b[u], numer[:, u].rearrange("p m t -> p (m t)"), inv[:, u].rearrange("p m t -> p (m t)"), ALU.mult
                )
            for u in (u0, u0 + 1):
                nc.vector.quantize_mx(z_w[:, P * u : P * (u + 1)].bitcast(FP8X4), z_s[:, P * u : P * (u + 1)], z_b[u])

        make_z(0)
        for c0, c1 in halves:
            nc.vector.quantize_mx(z2_w[:, c0:c1].bitcast(FP8X4), z2_s[:, c0:c1], z2_flat[:, TILES * c0 : TILES * c1])
        make_z(2)

        for u, c0, c1 in [(0, c0, c1) for c0, c1 in halves] + [(u, 0, V) for u in range(1, TILES)]:
            bank = psum.tile([P, BANK], F32, name="bank")
            nc.tensor.matmul_mx(
                out=bank[:, : c1 - c0],
                lhsT=z_w[:, P * u : P * (u + 1)].bitcast(FP8X4),
                lhsT_scale=z_s[:, P * u : P * (u + 1)],
                rhs=z2_w[:, c0:c1].bitcast(FP8X4),
                rhs_scale=z2_s[:, c0:c1],
                start=True,
                stop=True,
            )
            nc.scalar.mul(s_win[u][:, c0:c1], bank[:, : c1 - c0], 0.0625)

        s5 = sb("s5", [P, TILES, V], F32)
        res = sb("res", [P, TILES, V], F32)
        res_b = sb("res_b", [P, V, TILES], BF16)
        res_w = sb("res_w", [P, V], U32)
        res_s = sb("res_s", [P, V], U8)
        out_rows = out_0.rearrange("(p u) v -> p u v", u=TILES)
        out_words = out_1[0].rearrange("p v r -> p (v r)").bitcast(I32)

        for u0, c0, c1 in ((0, 0, V), (2, 0, FIRST), (2, FIRST, V)):
            entries = slice(c0 // LIST, c1 // LIST)
            for u in (u0, u0 + 1):
                nc.vector.tensor_copy(s5[:, u, c0:c1], s_win[u][:].indirect(n5_t[:, entries]))
            for u in (u0, u0 + 1):
                nc.vector.tensor_tensor(res[:, u, c0:c1], s_win[u][:].indirect(n6_t[:, entries]), s5[:, u, c0:c1], ALU.mult)
            nc.sync.dma_start(out_rows[:, u0 : u0 + 2, c0:c1], res[:, u0 : u0 + 2, c0:c1])
            nc.scalar.copy(
                res_b[:, c0:c1, u0 : u0 + 2].rearrange("p (c i) u -> p c u i", i=4),
                res[:, u0 : u0 + 2, c0:c1].rearrange("p u (c i) -> p c u i", i=4),
            )

        def quantize_res(c0, c1):
            nc.vector.quantize_mx(
                res_w[:, c0:c1].bitcast(FP8X4), res_s[:, c0:c1], res_b[:, c0:c1, :].rearrange("p v u -> p (v u)")
            )

        quantize_res(0, V // 2)
        quantize_res(V // 2, FIRST)
        nc.sync.dma_start(out_words[:, 0:FIRST], res_w[:, 0:FIRST].bitcast(I32))
        quantize_res(FIRST, V)
        nc.sync.dma_start(out_words[:, FIRST:], res_w[:, FIRST:].bitcast(I32))
        for q in range(QUADS):
            queue = nc.scalar if q % 2 else nc.sync
            queue.dma_start(out_2[0, 4 * q : 4 * q + 4, :].bitcast(I32), res_s[32 * q : 32 * q + 4, :].bitcast(I32))
